import numpy as np
import ml_dtypes


def mxq(x, axis, fmt="e4m3"):
    dtype, down = {"e4m3": (ml_dtypes.float8_e4m3fn, 7), "e5m2": (ml_dtypes.float8_e5m2, 14)}[fmt]
    v = np.moveaxis(np.asarray(x, np.float32).astype(ml_dtypes.bfloat16).astype(np.float64), axis, -1)
    blocks = v.reshape(v.shape[:-1] + (-1, 32))
    amax = np.abs(blocks).max(-1, keepdims=True)
    byte = np.maximum(np.where(amax > 0, np.frexp(amax)[1] - 1 + 127, 0) - down, 1)
    scale = np.exp2(byte - 127.0)
    codes = (blocks / scale).astype(np.float32).astype(dtype).astype(np.float64)
    return np.moveaxis((codes * scale).reshape(v.shape), -1, axis)


WIDE = False


def mx_kscale(k):
    if not WIDE:
        return np.ones(k)
    levels = np.array([10, -10, 5, -5, 0])
    if k % 512:
        return np.exp2(np.random.permutation(np.resize(levels, k // 32))).repeat(32)
    a = np.empty((k // 512, 16))
    for p in range(k // 512):
        a[p, :8] = np.random.permutation(np.resize(levels, 8))
        for g in range(8):
            far = levels[np.abs(levels - a[p, g]) >= 10]
            a[p, g + 8] = far[np.random.randint(len(far))]
    return np.exp2(a.ravel()).repeat(32)


def f64(x):
    return np.asarray(x).astype(np.float64)


def striped(idx):
    return np.tile(idx.reshape(-1, 16).T, (8, 1)).astype(np.uint16)


def unstriped(offs):
    return offs[:16].T.reshape(-1).astype(np.int64)


def pack_weight(w):
    k, n = w.shape
    w = f64(np.asarray(w, np.float32).astype(ml_dtypes.bfloat16)).reshape(k // 32, 32, n)
    amax = np.abs(w).max(1)
    byte = np.clip(np.where(amax > 0, np.frexp(amax)[1] - 1 + 127 - 7, 1), 1, 254)
    scaled = (w * np.exp2(127.0 - byte)[:, None, :]).reshape(k, n).astype(np.float32)
    words = np.ascontiguousarray(scaled.reshape(k // 512, 128, 4, n).transpose(0, 1, 3, 2)).astype(ml_dtypes.float8_e4m3fn).view(np.uint8)
    return words, np.ascontiguousarray(byte.astype(np.uint8).reshape(k // 512, 16, n))


def unpack_weight(words, scales):
    g, p, n, _ = words.shape
    vals = np.ascontiguousarray(words).view(ml_dtypes.float8_e4m3fn).astype(np.float64) * np.repeat(np.exp2(scales.astype(np.float64) - 127.0), 8, axis=1)[..., None]
    return vals.transpose(0, 1, 3, 2).reshape(g * 512, n)


K, T, S, N, U = 512, 1024, 512, 256, 1024


def setup_inputs():
    n = np.random.standard_normal
    s = mx_kscale(K)[:, None]
    packed_xT = pack_weight(n((K, T)) * s)
    return {
        "x_words": packed_xT[0],
        "x_scales": packed_xT[1],
        "w1": (n((K, N)) / np.sqrt(K) / s).astype(np.float32),
        "w2": (n((K, N)) / np.sqrt(K) / s).astype(np.float32),
        "w3": (n((K, N)) / np.sqrt(K) / s).astype(np.float32),
        "qm": (np.random.uniform(0.3, 0.8, (N, 1))).astype(np.float32),
        "velx": (n((N, U))).astype(np.float32),
        "vely": (n((N, U))).astype(np.float32),
        "offs": striped(np.random.permutation(T)[:S]),
        "cell": striped(np.random.permutation(np.concatenate([np.arange(S), np.random.randint(0, S, U - S)]))),
    }


def reference(x_words, x_scales, w1, w2, w3, qm, velx, vely, offs, cell):
    xq = unpack_weight(x_words, x_scales)[:, unstriped(offs)]
    ex = mxq(f64(w1), 0, "e4m3").T @ xq
    gx = ex[:, unstriped(cell)]
    ax = f64(qm) * gx
    vx = f64(velx) + ax
    ey = mxq(f64(w2), 0, "e4m3").T @ xq
    gy = ey[:, unstriped(cell)]
    ay = f64(qm) * gy
    vy = f64(vely) + ay
    bz = mxq(f64(w3), 0, "e4m3").T @ xq
    tz = bz[:, unstriped(cell)]
    tw = f64(qm) * tz
    wy = vy - (vx * tw)
    sw = (2.0 * tw) / ((tw) ** 2 + 1.0)
    nx = vx + wy * sw + ax
    wx = vx + vy * tw
    ny = vy - (wx * sw) + ay
    return 0.5 * ((nx) ** 2 + (ny) ** 2)

from contextlib import ExitStack
import math

import concourse.mybir as mybir

F32 = mybir.dt.float32
BF16 = mybir.dt.bfloat16
I32 = mybir.dt.int32
U32 = mybir.dt.uint32
U16 = mybir.dt.uint16
U8 = mybir.dt.uint8
FP8X4 = mybir.dt.float8_e4m3fn_x4
ALU = mybir.AluOpType
ACT = mybir.ActivationFunctionType

P = 128
K, T, S, N, U = 512, 1024, 512, 256, 1024
PACK = 4
BLOCKS = N // P
SPARE = 32
FLOPS = 3 * 2 * K * N * S
CHUNKS = [[512, 512], [512, 256, 256]]


def tile_picked_yboris_en_p_kernel(tc, x_words, x_scales, w1, w2, w3, qm, velx, vely, offs, cell, out):
    nc = tc.nc
    with ExitStack() as ctx:
        keep = ctx.enter_context(tc.tile_pool(name="keep", bufs=1))
        ring = ctx.enter_context(tc.tile_pool(name="ring", bufs=3))
        psum = ctx.enter_context(tc.psum_pool(name="psum", bufs=1))

        warm = keep.tile([P, 1], F32, name="warm")
        warm2 = keep.tile([P, 1], F32, name="warm2")
        nc.vector.memset(warm[:], 1.0)
        nc.scalar.activation(warm2[:], warm[:], ACT.Abs_reciprocal_sqrt)

        offs_t = keep.tile([P, S // 16], U16, name="offs_t")
        cell_t = keep.tile([P, U // 16], U16, name="cell_t")
        words = keep.tile([P, T], I32, name="words")
        scales = keep.tile([P, T], U8, name="scales")
        nc.gpsimd.memset(scales[:].bitcast(I32), 0)
        nc.sync.dma_start(out=words[:], in_=x_words[0].rearrange("p n t -> p (n t)").bitcast(I32))
        nc.sync.dma_start(offs_t[:], offs)
        for q in range(4):
            nc.sync.dma_start(out=scales[32 * q : 32 * q + 4, :].bitcast(I32), in_=x_scales[0][4 * q : 4 * q + 4, :].bitcast(I32))
        raw = {}
        for name, w in (("b", w3), ("y", w2), ("x", w1)):
            raw[name] = keep.tile([P, PACK, N], F32, name="raw_" + name)
            nc.sync.dma_start(out=raw[name][:], in_=w.rearrange("(p j) m -> p j m", j=PACK))
        q_t = keep.tile([P, BLOCKS, 1], F32, name="q_t")
        with nc.allow_non_contiguous_dma(reason="one value a partition"):
            nc.sync.dma_start(out=q_t[:], in_=qm.rearrange("(b p) o -> p b o", p=P))
        nc.sync.dma_start(cell_t[:], cell)
        vel = {}
        for b in range(BLOCKS):
            for name, v in (("x", velx), ("y", vely)):
                vel[name, b] = keep.tile([P, U], F32, name="vel_%s%d" % (name, b))
                nc.sync.dma_start(out=vel[name, b][:], in_=v[b * P : (b + 1) * P, :])

        x_codes = keep.tile([P, S], U32, name="x_codes", align_bytes=64)
        x_bytes = keep.tile([P, S], U8, name="x_bytes", align_bytes=64)
        nc.vector.tensor_copy(x_codes[:], words[:].bitcast(U32).indirect(offs_t[:]))
        nc.vector.tensor_copy(x_bytes[:], scales[:].indirect(offs_t[:]))

        field = {}
        for b in range(BLOCKS):
            for name in ("b", "y", "x"):
                grouped = keep.tile([P, P, PACK], BF16, name="grp_%s%d" % (name, b), align_bytes=64)
                src = raw[name][:, :, b * P : (b + 1) * P].rearrange("p j (c i) -> p c j i", i=4)
                dst = grouped[:].rearrange("p (c i) j -> p c j i", i=4)
                nc.scalar.copy(dst, src)
                codes = keep.tile([P, P], U32, name="wc_%s%d" % (name, b), align_bytes=64)
                wsc = keep.tile([P, P], U8, name="ws_%s%d" % (name, b), align_bytes=64)
                nc.vector.quantize_mx(out=codes[:].bitcast(FP8X4), scales=wsc[:], in_=grouped[:].rearrange("p c j -> p (c j)"))
                field[name, b] = psum.tile([P, S], F32, name="f_%s%d" % (name, b))
                nc.tensor.matmul_mx(out=field[name, b][:], lhsT=codes[:].bitcast(FP8X4), lhsT_scale=wsc[:],
                                    rhs=x_codes[:].bitcast(FP8X4), rhs_scale=x_bytes[:], start=True, stop=True)

        kick = {}
        for b in range(BLOCKS):
            q = q_t[:, b, :]
            ex, ey, bz = field["x", b], field["y", b], field["b", b]
            dx = keep.tile([P, S + SPARE], F32, name="dx%d" % b)
            dy = keep.tile([P, S + SPARE], F32, name="dy%d" % b)
            nc.gpsimd.memset(dx[:, S:], 0.0)
            nc.gpsimd.memset(dy[:, S:], 0.0)
            tt = keep.tile([P, S], F32, name="tt%d" % b)
            h = keep.tile([P, S], F32, name="h%d" % b)
            g = keep.tile([P, S], F32, name="g%d" % b)
            ay = keep.tile([P, S], F32, name="ay%d" % b)
            p1 = keep.tile([P, S], F32, name="p1%d" % b)
            uu = keep.tile([P, S], F32, name="uu%d" % b)
            p2 = keep.tile([P, S], F32, name="p2%d" % b)
            nc.scalar.activation(tt[:], bz[:], ACT.Square, scale=q)
            nc.scalar.activation(ay[:], ey[:], ACT.Copy, scale=q)
            nc.scalar.activation(h[:], tt[:], ACT.Abs_reciprocal_sqrt, bias=1.0)
            nc.scalar.activation(g[:], h[:], ACT.Square, scale=math.sqrt(2.0))
            halves = (slice(0, S // 2), slice(S // 2, S))
            for c in halves:
                nc.vector.scalar_tensor_tensor(p1[:, c], bz[:, c], q, ay[:, c], ALU.mult, ALU.mult)
            for c in halves:
                nc.vector.scalar_tensor_tensor(uu[:, c], ex[:, c], q, p1[:, c], ALU.mult, ALU.subtract)
            for c in halves:
                nc.vector.tensor_tensor(dx[:, c], uu[:, c], g[:, c], ALU.mult)
            for c in halves:
                nc.vector.scalar_tensor_tensor(p2[:, c], bz[:, c], q, dx[:, c], ALU.mult, ALU.mult)
            for c in halves:
                nc.vector.scalar_tensor_tensor(dy[:, c], ay[:, c], 2.0, p2[:, c], ALU.mult, ALU.add)
            kick["x", b], kick["y", b] = dx, dy

        for b in range(BLOCKS):
            r0 = 0
            for n in CHUNKS[b]:
                cols = slice(r0, r0 + n)
                lst = cell_t[:, r0 // 16 : (r0 + n) // 16]
                sq = {}
                for name in ("x", "y"):
                    moved = ring.tile([P, n], F32, name="moved_" + name)
                    nc.vector.tensor_tensor(moved[:], kick[name, b][:].indirect(lst), vel[name, b][:, cols], ALU.add)
                    sq[name] = ring.tile([P, n], F32, name="sq_" + name)
                    nc.scalar.activation(sq[name][:], moved[:], ACT.Square, scale=math.sqrt(0.5))
                res = ring.tile([P, n], F32, name="res")
                nc.vector.tensor_tensor(res[:], sq["x"][:], sq["y"][:], ALU.add)
                nc.sync.dma_start(out=out[b * P : (b + 1) * P, cols], in_=res[:])
                r0 = r0 + n
